import numpy as np
import ml_dtypes


def mxq(x, axis, fmt="e4m3"):
    dtype, down = {"e4m3": (ml_dtypes.float8_e4m3fn, 7), "e5m2": (ml_dtypes.float8_e5m2, 14)}[fmt]
    v = np.moveaxis(np.asarray(x, np.float32).astype(ml_dtypes.bfloat16).astype(np.float64), axis, -1)
    blocks = v.reshape(v.shape[:-1] + (-1, 32))
    amax = np.abs(blocks).max(-1, keepdims=True)
    byte = np.maximum(np.where(amax > 0, np.frexp(amax)[1] - 1 + 127, 0) - down, 1)
    scale = np.exp2(byte - 127.0)
    codes = (blocks / scale).astype(np.float32).astype(dtype).astype(np.float64)
    return np.moveaxis((codes * scale).reshape(v.shape), -1, axis)


WIDE = False


def mx_kscale(k):
    if not WIDE:
        return np.ones(k)
    levels = np.array([30, -30])
    if k % 512:
        return np.exp2(np.random.permutation(np.resize(levels, k // 32))).repeat(32)
    a = np.empty((k // 512, 16))
    for p in range(k // 512):
        a[p, :8] = np.random.permutation(np.resize(levels, 8))
        for g in range(8):
            far = levels[np.abs(levels - a[p, g]) >= 10]
            a[p, g + 8] = far[np.random.randint(len(far))]
    return np.exp2(a.ravel()).repeat(32)


def f64(x):
    return np.asarray(x).astype(np.float64)


def striped(idx):
    return np.tile(np.asarray(idx).reshape(-1, 16).T, (8, 1)).astype(np.uint16)


def unstriped(offs):
    return offs[:16].T.reshape(-1).astype(np.int64)


E2M1 = np.array([0.0, 0.5, 1.0, 1.5, 2.0, 3.0, 4.0, 6.0, -0.0, -0.5, -1.0, -1.5, -2.0, -3.0, -4.0, -6.0])


def pack_weight(w, fmt):
    k, n = w.shape
    w = f64(np.asarray(w, np.float32).astype(ml_dtypes.bfloat16)).reshape(k // 32, 32, n)
    amax = np.abs(w).max(1)
    if fmt in ("e4m3", "e5m2"):
        byte = np.frexp(amax)[1] - 1 + 127 - (7 if fmt == "e4m3" else 14)
    else:
        mant, ex = np.frexp(amax / 6.0)
        byte = np.where(mant > 0.5, ex, ex - 1) + 127
    byte = np.clip(np.where(amax > 0, byte, 1), 1, 254)
    scaled = (w * np.exp2(127.0 - byte)[:, None, :]).reshape(k, n).astype(np.float32)
    by_word = np.ascontiguousarray(scaled.reshape(k // 512, 128, 4, n).transpose(0, 1, 3, 2))
    if fmt in ("e4m3", "e5m2"):
        words = by_word.astype(ml_dtypes.float8_e4m3fn if fmt == "e4m3" else ml_dtypes.float8_e5m2).view(np.uint8)
    else:
        c = by_word.astype(ml_dtypes.float4_e2m1fn).view(np.uint8) & 0xF
        words = (c[..., 0::2] | (c[..., 1::2] << 4)).reshape(k // 512, 128, 2 * n)
    return np.ascontiguousarray(words), np.ascontiguousarray(byte.astype(np.uint8).reshape(k // 512, 16, n))


def unpack_weight(words, scales, fmt):
    g, _, n = scales.shape
    words = np.ascontiguousarray(words).reshape(g, 128, n, -1)
    if fmt in ("e4m3", "e5m2"):
        vals = words.view(ml_dtypes.float8_e4m3fn if fmt == "e4m3" else ml_dtypes.float8_e5m2).astype(np.float64)
    else:
        nib = np.empty((g, 128, n, 4), np.uint8)
        nib[..., 0::2] = words & 0xF
        nib[..., 1::2] = words >> 4
        vals = E2M1[nib]
    vals = vals * np.repeat(np.exp2(scales.astype(np.float64) - 127.0), 8, axis=1)[..., None]
    return vals.transpose(0, 1, 3, 2).reshape(g * 512, n)


K, T, Z, J, R, V, N, E = 512, 1024, 1024, 256, 512, 512, 256, 128


def setup_inputs():
    n = np.random.standard_normal
    idx = np.random.permutation(T)[:J]
    idx2 = np.random.permutation(Z)[:J]
    idx3 = np.random.permutation(V)[:J]
    idx4 = np.random.permutation(V)[:J]
    idx5 = np.random.permutation(J)[:E]
    idx6 = np.random.permutation(J)[:E]
    fk = mx_kscale(K)
    fr = mx_kscale(R)
    xtp = pack_weight(n((K, T)) / fk[:, None], "e4m3")
    xop = pack_weight(n((K, Z)) / fk[:, None], "e2m1")
    wp = pack_weight(n((K, R)) * 1 / np.sqrt(K) * fk[:, None] * fr, "e5m2")
    w2p = pack_weight(n((K, R)) * 1 / np.sqrt(K) * fk[:, None] * fr, "e5m2")
    wbp = pack_weight(n((R, N)) * 1 / np.sqrt(R) / fr[:, None], "e5m2")
    return {
        "xt_words": xtp[0],
        "xt_scales": xtp[1],
        "xo_words": xop[0],
        "xo_scales": xop[1],
        "w_words": wp[0],
        "w_scales": wp[1],
        "w2_words": w2p[0],
        "w2_scales": w2p[1],
        "tb": (n((R, V)) * 0.8 * fr[:, None]).astype(np.float32),
        "wb_words": wbp[0],
        "wb_scales": wbp[1],
        "offs": striped(idx),
        "offs2": striped(idx2),
        "offs3": striped(idx3),
        "offs4": striped(idx4),
        "offs5": striped(idx5),
        "offs6": striped(idx6),
    }


def reference(xt_words, xt_scales, xo_words, xo_scales, w_words, w_scales, w2_words, w2_scales, tb, wb_words, wb_scales, offs, offs2, offs3, offs4, offs5, offs6):
    idx = unstriped(offs)
    idx2 = unstriped(offs2)
    idx3 = unstriped(offs3)
    idx4 = unstriped(offs4)
    idx5 = unstriped(offs5)
    idx6 = unstriped(offs6)
    xtu = unpack_weight(xt_words, xt_scales, "e4m3")
    xou = unpack_weight(xo_words, xo_scales, "e2m1")
    wu = unpack_weight(w_words, w_scales, "e5m2")
    w2u = unpack_weight(w2_words, w2_scales, "e5m2")
    wbu = unpack_weight(wb_words, wb_scales, "e5m2")
    xtidxg = xtu[:, idx]
    xoidx2g = xou[:, idx2]
    a = wu.T @ xtidxg + w2u.T @ xoidx2g
    b = w2u.T @ xtidxg + wu.T @ xoidx2g
    hid = np.maximum(a + f64(tb)[:, idx3], b + f64(tb)[:, idx4])
    hidq = mxq(hid, 0, "e4m3")
    p = wbu.T @ hidq
    y = np.maximum(p[:, idx5], p[:, idx6])
    return y

@@ -1,0 +1,195 @@
+from contextlib import ExitStack
+
+import concourse.mybir as mybir
+
+K, T, Z, J, R, V, N, E = 512, 1024, 1024, 256, 512, 512, 256, 128
+FLOPS = 2 * (4 * K * R * J + R * N * J)
+
+F32 = mybir.dt.float32
+BF16 = mybir.dt.bfloat16
+I32 = mybir.dt.int32
+U32 = mybir.dt.uint32
+U16 = mybir.dt.uint16
+U8 = mybir.dt.uint8
+E4M3 = mybir.dt.float8_e4m3fn_x4
+E5M2 = mybir.dt.float8_e5m2_x4
+E2M1 = mybir.dt.float4_e2m1fn_x4
+ADD = mybir.AluOpType.add
+MAX = mybir.AluOpType.max
+COPY = mybir.ActivationFunctionType.Copy
+
+P = 128
+PACK = 4
+
+
+def load_low_scales(queue, plane, rows):
+    queue.dma_start(out=plane[0:16, :].bitcast(I32), in_=rows[0].bitcast(I32))
+
+
+def load_high_scales(queue, plane, rows):
+    queue.dma_start(out=plane[16:P, :].bitcast(I32), in_=rows[0, 2:16, :].bitcast(I32).partition_broadcast(8))
+
+
+def load_words(queue, tile, words):
+    queue.dma_start(out=tile.bitcast(I32), in_=words.bitcast(I32))
+
+
+def tile_list_levelled_crossed_one_bestoftwo_kernel(
+    tc, xt_words, xt_scales, xo_words, xo_scales, w_words, w_scales, w2_words, w2_scales, tb,
+    wb_words, wb_scales, offs, offs2, offs3, offs4, offs5, offs6, out,
+):
+    nc = tc.nc
+    with ExitStack() as ctx:
+        lists = ctx.enter_context(tc.tile_pool(name="lists", bufs=1))
+        sb = ctx.enter_context(tc.tile_pool(name="sb", bufs=1))
+        psum = ctx.enter_context(tc.psum_pool(name="psum", bufs=1))
+
+        idx = lists.tile([P, J // 16], U16, name="idx")
+        idx2 = lists.tile([P, J // 16], U16, name="idx2")
+        idx3 = lists.tile([P, J // 16], U16, name="idx3")
+        idx4 = lists.tile([P, J // 16], U16, name="idx4")
+        idx5 = lists.tile([P, E // 16], U16, name="idx5")
+        idx6 = lists.tile([P, E // 16], U16, name="idx6")
+
+        xt_w = sb.tile([P, T], U32, name="xt_w", align_bytes=64)
+        xt_s = sb.tile([P, T], U8, name="xt_s", align_bytes=64)
+        xo_w = sb.tile([P, Z], U16, name="xo_w", align_bytes=64)
+        xo_s = sb.tile([P, Z], U8, name="xo_s", align_bytes=64)
+        w_raw = [sb.tile([P, R], U32, name=f"w_raw{m}", align_bytes=64) for m in range(2)]
+        ws_raw = [sb.tile([P, R], U8, name=f"ws_raw{m}", align_bytes=64) for m in range(2)]
+        w_w = [sb.tile([P, R], U32, name=f"w_w{m}", align_bytes=64) for m in range(2)]
+        w_s = [sb.tile([P, R], U8, name=f"w_s{m}", align_bytes=64) for m in range(2)]
+        wb_w = sb.tile([P, N], U32, name="wb_w", align_bytes=64)
+        wb_s = sb.tile([P, N], U8, name="wb_s", align_bytes=64)
+        levels = [sb.tile([P, V], F32, name=f"levels{t}") for t in range(PACK)]
+
+        tb_rows = tb.rearrange("(p t) v -> p t v", t=PACK)
+        load_high_scales(nc.gpsimd, xt_s, xt_scales)
+        load_high_scales(nc.gpsimd, xo_s, xo_scales)
+        load_low_scales(nc.scalar, xt_s, xt_scales)
+        load_low_scales(nc.scalar, ws_raw[0], w_scales)
+        load_low_scales(nc.scalar, ws_raw[1], w2_scales)
+        load_high_scales(nc.scalar, ws_raw[0], w_scales)
+        load_high_scales(nc.scalar, ws_raw[1], w2_scales)
+        nc.sync.dma_start(idx3[:], offs3)
+        nc.sync.dma_start(out=levels[0][:], in_=tb_rows[:, 0, :])
+        nc.sync.dma_start(idx[:], offs)
+        load_words(nc.sync, xt_w[:], xt_words[0].rearrange("p c b -> p (c b)"))
+        load_words(nc.sync, w_raw[0][:], w_words[0].rearrange("p c b -> p (c b)"))
+        nc.sync.dma_start(idx4[:], offs4)
+        load_words(nc.sync, w_raw[1][:], w2_words[0].rearrange("p c b -> p (c b)"))
+        nc.sync.dma_start(idx2[:], offs2)
+        load_words(nc.sync, xo_w[:], xo_words[0])
+        load_low_scales(nc.sync, xo_s, xo_scales)
+        for t in range(1, PACK):
+            nc.sync.dma_start(out=levels[t][:], in_=tb_rows[:, t, :])
+        load_words(nc.sync, wb_w[:], wb_words[0].rearrange("p c b -> p (c b)"))
+        load_low_scales(nc.sync, wb_s, wb_scales)
+        load_high_scales(nc.sync, wb_s, wb_scales)
+        nc.sync.dma_start(idx5[:], offs5)
+        nc.sync.dma_start(idx6[:], offs6)
+
+        xt_gw = sb.tile([P, J], U32, name="xt_gw", align_bytes=64)
+        xt_gs = sb.tile([P, J], U8, name="xt_gs", align_bytes=64)
+        xo_gw = sb.tile([P, J], U16, name="xo_gw", align_bytes=64)
+        xo_gs = sb.tile([P, J], U8, name="xo_gs", align_bytes=64)
+
+        def deal(dst, src):
+            nc.vector.tensor_copy(
+                out=dst[:].rearrange("p (t m) -> p m t", t=PACK),
+                in_=src[:].rearrange("p (m t) -> p m t", t=PACK),
+            )
+
+        nc.vector.tensor_copy(xt_gw[:], xt_w[:].indirect(idx[:]))
+        nc.vector.tensor_copy(xt_gs[:], xt_s[:].indirect(idx[:]))
+        for m in range(2):
+            deal(w_w[m], w_raw[m])
+            nc.gpsimd.tensor_copy(
+                out=w_s[m][:].rearrange("p (t m) -> p t m", t=PACK),
+                in_=ws_raw[m][:].rearrange("p (m t) -> p t m", t=PACK),
+            )
+        nc.vector.tensor_copy(xo_gw[:], xo_w[:].indirect(idx2[:]))
+        nc.vector.tensor_copy(xo_gs[:], xo_s[:].indirect(idx2[:]))
+
+        picked = [sb.tile([P, 2, J], F32, name=f"picked{t}") for t in range(PACK)]
+        for t in range(PACK):
+            nc.scalar.activation(picked[t][:, 0, :], levels[t][:].indirect(idx3[:]), COPY)
+            nc.scalar.activation(picked[t][:, 1, :], levels[t][:].indirect(idx4[:]), COPY)
+
+        banks = [psum.tile([P, 2, J], F32, name=f"ab{t}") for t in range(PACK)]
+
+        def mx_pass(t, half, m, words, scales, start, stop):
+            cols = slice(P * t, P * (t + 1))
+            nc.tensor.matmul_mx(
+                out=banks[t][:, half, :],
+                lhsT=w_w[m][:, cols].bitcast(E5M2),
+                lhsT_scale=w_s[m][:, cols],
+                rhs=words,
+                rhs_scale=scales,
+                start=start,
+                stop=stop,
+            )
+
+        for t in range(PACK):
+            mx_pass(t, 0, 0, xt_gw[:].bitcast(E4M3), xt_gs[:], True, False)
+        for t in range(PACK):
+            mx_pass(t, 1, 1, xt_gw[:].bitcast(E4M3), xt_gs[:], False, False)
+            for m in range(2):
+                mx_pass(t, 1 - m, m, xo_gw[:].bitcast(E2M1), xo_gs[:], False, m == 1)
+
+        hid = sb.tile([P, J, PACK], BF16, name="hid", align_bytes=64)
+        sums = [sb.tile([P, 2, 2, J], F32, name=f"sums{pair}") for pair in range(2)]
+
+        def keep_larger(pair, cols):
+            nc.vector.tensor_tensor(
+                hid[:, cols, 2 * pair : 2 * pair + 2],
+                sums[pair][:, :, 0, cols].rearrange("p u j -> p j u"),
+                sums[pair][:, :, 1, cols].rearrange("p u j -> p j u"),
+                MAX,
+            )
+
+        halves = [slice(0, J // 2), slice(J // 2, J)]
+        for t in range(PACK):
+            nc.vector.tensor_tensor(sums[t // 2][:, t % 2], banks[t][:], picked[t][:], ADD)
+            if t == 1:
+                keep_larger(0, slice(0, J))
+        for cols in halves:
+            keep_larger(1, cols)
+
+        hid_w = sb.tile([P, J], U32, name="hid_w", align_bytes=64)
+        hid_s = sb.tile([P, J], U8, name="hid_s", align_bytes=64)
+        p_sb = [sb.tile([P, J], F32, name=f"p_sb{c}") for c in range(2)]
+        for h, cols in enumerate(halves):
+            nc.vector.quantize_mx(
+                out=hid_w[:, cols].bitcast(E4M3),
+                scales=hid_s[:, cols],
+                in_=hid[:, cols, :].rearrange("p j t -> p (j t)"),
+            )
+        for h, cols in enumerate(halves):
+            for c in range(2):
+                rows = slice(P * c, P * (c + 1))
+                p_bank = psum.tile([P, J // 2], F32, name=f"p_bank{h}{c}")
+                nc.tensor.matmul_mx(
+                    out=p_bank[:],
+                    lhsT=wb_w[:, rows].bitcast(E5M2),
+                    lhsT_scale=wb_s[:, rows],
+                    rhs=hid_w[:, cols].bitcast(E4M3),
+                    rhs_scale=hid_s[:, cols],
+                    start=True,
+                    stop=True,
+                )
+                if c == 1 and h == 1:
+                    nc.vector.tensor_copy(p_sb[c][:, cols], p_bank[:])
+                else:
+                    nc.scalar.copy(p_sb[c][:, cols], p_bank[:])
+
+        by5 = [sb.tile([P, E], F32, name=f"by5_{c}") for c in range(2)]
+        by6 = [sb.tile([P, E], F32, name=f"by6_{c}") for c in range(2)]
+        best = [sb.tile([P, E], F32, name=f"best{c}") for c in range(2)]
+        nc.scalar.activation(by5[0][:], p_sb[0][:].indirect(idx5[:]), COPY)
+        nc.scalar.activation(by6[0][:], p_sb[0][:].indirect(idx6[:]), COPY)
+        nc.vector.tensor_copy(by5[1][:], p_sb[1][:].indirect(idx5[:]))
+        nc.vector.tensor_copy(by6[1][:], p_sb[1][:].indirect(idx6[:]))
+        for c, queue in enumerate((nc.sync, nc.scalar)):
+            nc.vector.tensor_tensor(best[c][:], by5[c][:], by6[c][:], MAX)
+            queue.dma_start(out=out[P * c : P * (c + 1), :], in_=best[c][:])

@@ -68,21 +68,22 @@ def tile_list_levelled_crossed_one_bestoftwo_kernel(
         load_high_scales(nc.gpsimd, xo_s, xo_scales)
         load_low_scales(nc.scalar, xt_s, xt_scales)
         load_low_scales(nc.scalar, ws_raw[0], w_scales)
-        load_low_scales(nc.scalar, ws_raw[1], w2_scales)
+        load_low_scales(nc.scalar, xo_s, xo_scales)
         load_high_scales(nc.scalar, ws_raw[0], w_scales)
-        load_high_scales(nc.scalar, ws_raw[1], w2_scales)
         nc.sync.dma_start(idx3[:], offs3)
         nc.sync.dma_start(out=levels[0][:], in_=tb_rows[:, 0, :])
+        load_words(nc.sync, w_raw[0][:], w_words[0].rearrange("p c b -> p (c b)"))
         nc.sync.dma_start(idx[:], offs)
         load_words(nc.sync, xt_w[:], xt_words[0].rearrange("p c b -> p (c b)"))
-        load_words(nc.sync, w_raw[0][:], w_words[0].rearrange("p c b -> p (c b)"))
         nc.sync.dma_start(idx4[:], offs4)
-        load_words(nc.sync, w_raw[1][:], w2_words[0].rearrange("p c b -> p (c b)"))
         nc.sync.dma_start(idx2[:], offs2)
         load_words(nc.sync, xo_w[:], xo_words[0])
-        load_low_scales(nc.sync, xo_s, xo_scales)
-        for t in range(1, PACK):
-            nc.sync.dma_start(out=levels[t][:], in_=tb_rows[:, t, :])
+        load_high_scales(nc.sync, ws_raw[1], w2_scales)
+        load_low_scales(nc.sync, ws_raw[1], w2_scales)
+        nc.sync.dma_start(out=levels[1][:], in_=tb_rows[:, 1, :])
+        load_words(nc.sync, w_raw[1][:], w2_words[0].rearrange("p c b -> p (c b)"))
+        nc.sync.dma_start(out=levels[2][:], in_=tb_rows[:, 2, :])
+        nc.sync.dma_start(out=levels[3][:], in_=tb_rows[:, 3, :])
         load_words(nc.sync, wb_w[:], wb_words[0].rearrange("p c b -> p (c b)"))
         load_low_scales(nc.sync, wb_s, wb_scales)
         load_high_scales(nc.sync, wb_s, wb_scales)
@@ -100,16 +101,17 @@ def tile_list_levelled_crossed_one_bestoftwo_kernel(
                 in_=src[:].rearrange("p (m t) -> p m t", t=PACK),
             )
 
-        nc.vector.tensor_copy(xt_gw[:], xt_w[:].indirect(idx[:]))
+        deal(w_w[0], w_raw[0])
         nc.vector.tensor_copy(xt_gs[:], xt_s[:].indirect(idx[:]))
+        nc.vector.tensor_copy(xt_gw[:], xt_w[:].indirect(idx[:]))
+        nc.vector.tensor_copy(xo_gw[:], xo_w[:].indirect(idx2[:]))
+        nc.vector.tensor_copy(xo_gs[:], xo_s[:].indirect(idx2[:]))
+        deal(w_w[1], w_raw[1])
         for m in range(2):
-            deal(w_w[m], w_raw[m])
             nc.gpsimd.tensor_copy(
                 out=w_s[m][:].rearrange("p (t m) -> p t m", t=PACK),
                 in_=ws_raw[m][:].rearrange("p (m t) -> p t m", t=PACK),
             )
-        nc.vector.tensor_copy(xo_gw[:], xo_w[:].indirect(idx2[:]))
-        nc.vector.tensor_copy(xo_gs[:], xo_s[:].indirect(idx2[:]))
 
         picked = [sb.tile([P, 2, J], F32, name=f"picked{t}") for t in range(PACK)]
         for t in range(PACK):
@@ -133,9 +135,12 @@ def tile_list_levelled_crossed_one_bestoftwo_kernel(
         for t in range(PACK):
             mx_pass(t, 0, 0, xt_gw[:].bitcast(E4M3), xt_gs[:], True, False)
         for t in range(PACK):
+            if t < 2:
+                mx_pass(t, 1, 0, xo_gw[:].bitcast(E2M1), xo_gs[:], False, False)
             mx_pass(t, 1, 1, xt_gw[:].bitcast(E4M3), xt_gs[:], False, False)
-            for m in range(2):
-                mx_pass(t, 1 - m, m, xo_gw[:].bitcast(E2M1), xo_gs[:], False, m == 1)
+            if t >= 2:
+                mx_pass(t, 1, 0, xo_gw[:].bitcast(E2M1), xo_gs[:], False, False)
+            mx_pass(t, 0, 1, xo_gw[:].bitcast(E2M1), xo_gs[:], False, True)
 
         hid = sb.tile([P, J, PACK], BF16, name="hid", align_bytes=64)
         sums = [sb.tile([P, 2, 2, J], F32, name=f"sums{pair}") for pair in range(2)]
@@ -151,8 +156,8 @@ def tile_list_levelled_crossed_one_bestoftwo_kernel(
         halves = [slice(0, J // 2), slice(J // 2, J)]
         for t in range(PACK):
             nc.vector.tensor_tensor(sums[t // 2][:, t % 2], banks[t][:], picked[t][:], ADD)
-            if t == 1:
-                keep_larger(0, slice(0, J))
+            if t >= 2:
+                keep_larger(0, halves[t - 2])
         for cols in halves:
             keep_larger(1, cols)
 
@@ -166,7 +171,7 @@ def tile_list_levelled_crossed_one_bestoftwo_kernel(
                 in_=hid[:, cols, :].rearrange("p j t -> p (j t)"),
             )
         for h, cols in enumerate(halves):
-            for c in range(2):
+            for c in (1, 0):
                 rows = slice(P * c, P * (c + 1))
                 p_bank = psum.tile([P, J // 2], F32, name=f"p_bank{h}{c}")
                 nc.tensor.matmul_mx(

@@ -116,7 +116,10 @@ def tile_list_levelled_crossed_one_bestoftwo_kernel(
         picked = [sb.tile([P, 2, J], F32, name=f"picked{t}") for t in range(PACK)]
         for t in range(PACK):
             nc.scalar.activation(picked[t][:, 0, :], levels[t][:].indirect(idx3[:]), COPY)
-            nc.scalar.activation(picked[t][:, 1, :], levels[t][:].indirect(idx4[:]), COPY)
+            if t == 2:
+                nc.vector.tensor_copy(picked[t][:, 1, :], levels[t][:].indirect(idx4[:]))
+            else:
+                nc.scalar.activation(picked[t][:, 1, :], levels[t][:].indirect(idx4[:]), COPY)
 
         banks = [psum.tile([P, 2, J], F32, name=f"ab{t}") for t in range(PACK)]
 
@@ -143,23 +146,20 @@ def tile_list_levelled_crossed_one_bestoftwo_kernel(
             mx_pass(t, 0, 1, xo_gw[:].bitcast(E2M1), xo_gs[:], False, True)
 
         hid = sb.tile([P, J, PACK], BF16, name="hid", align_bytes=64)
-        sums = [sb.tile([P, 2, 2, J], F32, name=f"sums{pair}") for pair in range(2)]
-
-        def keep_larger(pair, cols):
+        sums = sb.tile([P, PACK, 2, J], F32, name="sums")
+        halves = [slice(0, J // 2), slice(J // 2, J)]
+        for t in range(PACK - 1):
+            nc.vector.tensor_tensor(sums[:, t], banks[t][:], picked[t][:], ADD)
+        for cols in halves:
+            t = PACK - 1
+            nc.vector.tensor_tensor(sums[:, t, :, cols], banks[t][:, :, cols], picked[t][:, :, cols], ADD)
+        for cols in halves:
             nc.vector.tensor_tensor(
-                hid[:, cols, 2 * pair : 2 * pair + 2],
-                sums[pair][:, :, 0, cols].rearrange("p u j -> p j u"),
-                sums[pair][:, :, 1, cols].rearrange("p u j -> p j u"),
+                hid[:, cols, :].rearrange("p (c i) t -> p c t i", i=4),
+                sums[:, :, 0, cols].rearrange("p t (c i) -> p c t i", i=4),
+                sums[:, :, 1, cols].rearrange("p t (c i) -> p c t i", i=4),
                 MAX,
             )
-
-        halves = [slice(0, J // 2), slice(J // 2, J)]
-        for t in range(PACK):
-            nc.vector.tensor_tensor(sums[t // 2][:, t % 2], banks[t][:], picked[t][:], ADD)
-            if t >= 2:
-                keep_larger(0, halves[t - 2])
-        for cols in halves:
-            keep_larger(1, cols)
 
         hid_w = sb.tile([P, J], U32, name="hid_w", align_bytes=64)
         hid_s = sb.tile([P, J], U8, name="hid_s", align_bytes=64)

from contextlib import ExitStack

import concourse.mybir as mybir

K, T, Z, J, R, V, N, E = 512, 1024, 1024, 256, 512, 512, 256, 128
FLOPS = 2 * (4 * K * R * J + R * N * J)

F32 = mybir.dt.float32
BF16 = mybir.dt.bfloat16
I32 = mybir.dt.int32
U32 = mybir.dt.uint32
U16 = mybir.dt.uint16
U8 = mybir.dt.uint8
E4M3 = mybir.dt.float8_e4m3fn_x4
E5M2 = mybir.dt.float8_e5m2_x4
E2M1 = mybir.dt.float4_e2m1fn_x4
ADD = mybir.AluOpType.add
MAX = mybir.AluOpType.max
COPY = mybir.ActivationFunctionType.Copy

P = 128
PACK = 4


def load_low_scales(queue, plane, rows):
    queue.dma_start(out=plane[0:16, :].bitcast(I32), in_=rows[0].bitcast(I32))


def load_high_scales(queue, plane, rows):
    queue.dma_start(out=plane[16:P, :].bitcast(I32), in_=rows[0, 2:16, :].bitcast(I32).partition_broadcast(8))


def load_words(queue, tile, words):
    queue.dma_start(out=tile.bitcast(I32), in_=words.bitcast(I32))


def tile_list_levelled_crossed_one_bestoftwo_kernel(
    tc, xt_words, xt_scales, xo_words, xo_scales, w_words, w_scales, w2_words, w2_scales, tb,
    wb_words, wb_scales, offs, offs2, offs3, offs4, offs5, offs6, out,
):
    nc = tc.nc
    with ExitStack() as ctx:
        lists = ctx.enter_context(tc.tile_pool(name="lists", bufs=1))
        sb = ctx.enter_context(tc.tile_pool(name="sb", bufs=1))
        psum = ctx.enter_context(tc.psum_pool(name="psum", bufs=1))

        idx = lists.tile([P, J // 16], U16, name="idx")
        idx2 = lists.tile([P, J // 16], U16, name="idx2")
        idx3 = lists.tile([P, J // 16], U16, name="idx3")
        idx4 = lists.tile([P, J // 16], U16, name="idx4")
        idx5 = lists.tile([P, E // 16], U16, name="idx5")
        idx6 = lists.tile([P, E // 16], U16, name="idx6")

        xt_w = sb.tile([P, T], U32, name="xt_w", align_bytes=64)
        xt_s = sb.tile([P, T], U8, name="xt_s", align_bytes=64)
        xo_w = sb.tile([P, Z], U16, name="xo_w", align_bytes=64)
        xo_s = sb.tile([P, Z], U8, name="xo_s", align_bytes=64)
        w_raw = [sb.tile([P, R], U32, name=f"w_raw{m}", align_bytes=64) for m in range(2)]
        ws_raw = [sb.tile([P, R], U8, name=f"ws_raw{m}", align_bytes=64) for m in range(2)]
        w_w = [sb.tile([P, R], U32, name=f"w_w{m}", align_bytes=64) for m in range(2)]
        w_s = [sb.tile([P, R], U8, name=f"w_s{m}", align_bytes=64) for m in range(2)]
        wb_w = sb.tile([P, N], U32, name="wb_w", align_bytes=64)
        wb_s = sb.tile([P, N], U8, name="wb_s", align_bytes=64)
        levels = [sb.tile([P, V], F32, name=f"levels{t}") for t in range(PACK)]

        tb_rows = tb.rearrange("(p t) v -> p t v", t=PACK)
        load_high_scales(nc.gpsimd, xt_s, xt_scales)
        load_high_scales(nc.gpsimd, xo_s, xo_scales)
        load_low_scales(nc.scalar, xt_s, xt_scales)
        load_low_scales(nc.scalar, ws_raw[0], w_scales)
        load_low_scales(nc.scalar, xo_s, xo_scales)
        load_high_scales(nc.scalar, ws_raw[0], w_scales)
        nc.sync.dma_start(idx3[:], offs3)
        nc.sync.dma_start(out=levels[0][:], in_=tb_rows[:, 0, :])
        load_words(nc.sync, w_raw[0][:], w_words[0].rearrange("p c b -> p (c b)"))
        nc.sync.dma_start(idx[:], offs)
        load_words(nc.sync, xt_w[:], xt_words[0].rearrange("p c b -> p (c b)"))
        nc.sync.dma_start(idx4[:], offs4)
        nc.sync.dma_start(idx2[:], offs2)
        load_words(nc.sync, xo_w[:], xo_words[0])
        load_high_scales(nc.sync, ws_raw[1], w2_scales)
        load_low_scales(nc.sync, ws_raw[1], w2_scales)
        nc.sync.dma_start(out=levels[1][:], in_=tb_rows[:, 1, :])
        load_words(nc.sync, w_raw[1][:], w2_words[0].rearrange("p c b -> p (c b)"))
        nc.sync.dma_start(out=levels[2][:], in_=tb_rows[:, 2, :])
        nc.sync.dma_start(out=levels[3][:], in_=tb_rows[:, 3, :])
        load_words(nc.sync, wb_w[:], wb_words[0].rearrange("p c b -> p (c b)"))
        load_low_scales(nc.sync, wb_s, wb_scales)
        load_high_scales(nc.sync, wb_s, wb_scales)
        nc.sync.dma_start(idx5[:], offs5)
        nc.sync.dma_start(idx6[:], offs6)

        xt_gw = sb.tile([P, J], U32, name="xt_gw", align_bytes=64)
        xt_gs = sb.tile([P, J], U8, name="xt_gs", align_bytes=64)
        xo_gw = sb.tile([P, J], U16, name="xo_gw", align_bytes=64)
        xo_gs = sb.tile([P, J], U8, name="xo_gs", align_bytes=64)

        def deal(dst, src):
            nc.vector.tensor_copy(
                out=dst[:].rearrange("p (t m) -> p m t", t=PACK),
                in_=src[:].rearrange("p (m t) -> p m t", t=PACK),
            )

        deal(w_w[0], w_raw[0])
        nc.vector.tensor_copy(xt_gs[:], xt_s[:].indirect(idx[:]))
        nc.vector.tensor_copy(xt_gw[:], xt_w[:].indirect(idx[:]))
        nc.vector.tensor_copy(xo_gw[:], xo_w[:].indirect(idx2[:]))
        nc.vector.tensor_copy(xo_gs[:], xo_s[:].indirect(idx2[:]))
        deal(w_w[1], w_raw[1])
        for m in range(2):
            nc.gpsimd.tensor_copy(
                out=w_s[m][:].rearrange("p (t m) -> p t m", t=PACK),
                in_=ws_raw[m][:].rearrange("p (m t) -> p t m", t=PACK),
            )

        picked = [sb.tile([P, 2, J], F32, name=f"picked{t}") for t in range(PACK)]
        for t in range(PACK):
            nc.scalar.activation(picked[t][:, 0, :], levels[t][:].indirect(idx3[:]), COPY)
            if t == 2:
                nc.vector.tensor_copy(picked[t][:, 1, :], levels[t][:].indirect(idx4[:]))
            else:
                nc.scalar.activation(picked[t][:, 1, :], levels[t][:].indirect(idx4[:]), COPY)

        banks = [psum.tile([P, 2, J], F32, name=f"ab{t}") for t in range(PACK)]

        def mx_pass(t, half, m, words, scales, start, stop):
            cols = slice(P * t, P * (t + 1))
            nc.tensor.matmul_mx(
                out=banks[t][:, half, :],
                lhsT=w_w[m][:, cols].bitcast(E5M2),
                lhsT_scale=w_s[m][:, cols],
                rhs=words,
                rhs_scale=scales,
                start=start,
                stop=stop,
            )

        for t in range(PACK):
            mx_pass(t, 0, 0, xt_gw[:].bitcast(E4M3), xt_gs[:], True, False)
        for t in range(PACK):
            if t < 2:
                mx_pass(t, 1, 0, xo_gw[:].bitcast(E2M1), xo_gs[:], False, False)
            mx_pass(t, 1, 1, xt_gw[:].bitcast(E4M3), xt_gs[:], False, False)
            if t >= 2:
                mx_pass(t, 1, 0, xo_gw[:].bitcast(E2M1), xo_gs[:], False, False)
            mx_pass(t, 0, 1, xo_gw[:].bitcast(E2M1), xo_gs[:], False, True)

        hid = sb.tile([P, J, PACK], BF16, name="hid", align_bytes=64)
        sums = sb.tile([P, PACK, 2, J], F32, name="sums")
        halves = [slice(0, J // 2), slice(J // 2, J)]
        for t in range(PACK - 1):
            nc.vector.tensor_tensor(sums[:, t], banks[t][:], picked[t][:], ADD)
        for cols in halves:
            t = PACK - 1
            nc.vector.tensor_tensor(sums[:, t, :, cols], banks[t][:, :, cols], picked[t][:, :, cols], ADD)
        for cols in halves:
            nc.vector.tensor_tensor(
                hid[:, cols, :].rearrange("p (c i) t -> p c t i", i=4),
                sums[:, :, 0, cols].rearrange("p t (c i) -> p c t i", i=4),
                sums[:, :, 1, cols].rearrange("p t (c i) -> p c t i", i=4),
                MAX,
            )

        hid_w = sb.tile([P, J], U32, name="hid_w", align_bytes=64)
        hid_s = sb.tile([P, J], U8, name="hid_s", align_bytes=64)
        p_sb = [sb.tile([P, J], F32, name=f"p_sb{c}") for c in range(2)]
        for h, cols in enumerate(halves):
            nc.vector.quantize_mx(
                out=hid_w[:, cols].bitcast(E4M3),
                scales=hid_s[:, cols],
                in_=hid[:, cols, :].rearrange("p j t -> p (j t)"),
            )
        for h, cols in enumerate(halves):
            for c in (1, 0):
                rows = slice(P * c, P * (c + 1))
                p_bank = psum.tile([P, J // 2], F32, name=f"p_bank{h}{c}")
                nc.tensor.matmul_mx(
                    out=p_bank[:],
                    lhsT=wb_w[:, rows].bitcast(E5M2),
                    lhsT_scale=wb_s[:, rows],
                    rhs=hid_w[:, cols].bitcast(E4M3),
                    rhs_scale=hid_s[:, cols],
                    start=True,
                    stop=True,
                )
                if c == 1 and h == 1:
                    nc.vector.tensor_copy(p_sb[c][:, cols], p_bank[:])
                else:
                    nc.scalar.copy(p_sb[c][:, cols], p_bank[:])

        by5 = [sb.tile([P, E], F32, name=f"by5_{c}") for c in range(2)]
        by6 = [sb.tile([P, E], F32, name=f"by6_{c}") for c in range(2)]
        best = [sb.tile([P, E], F32, name=f"best{c}") for c in range(2)]
        nc.scalar.activation(by5[0][:], p_sb[0][:].indirect(idx5[:]), COPY)
        nc.scalar.activation(by6[0][:], p_sb[0][:].indirect(idx6[:]), COPY)
        nc.vector.tensor_copy(by5[1][:], p_sb[1][:].indirect(idx5[:]))
        nc.vector.tensor_copy(by6[1][:], p_sb[1][:].indirect(idx6[:]))
        for c, queue in enumerate((nc.sync, nc.scalar)):
            nc.vector.tensor_tensor(best[c][:], by5[c][:], by6[c][:], MAX)
            queue.dma_start(out=out[P * c : P * (c + 1), :], in_=best[c][:])
